import numpy as np
import ml_dtypes


def mxq(x, axis, fmt="e4m3"):
    dtype, down = {"e4m3": (ml_dtypes.float8_e4m3fn, 7), "e5m2": (ml_dtypes.float8_e5m2, 14)}[fmt]
    v = np.moveaxis(np.asarray(x, np.float32).astype(ml_dtypes.bfloat16).astype(np.float64), axis, -1)
    blocks = v.reshape(v.shape[:-1] + (-1, 32))
    amax = np.abs(blocks).max(-1, keepdims=True)
    byte = np.maximum(np.where(amax > 0, np.frexp(amax)[1] - 1 + 127, 0) - down, 1)
    scale = np.exp2(byte - 127.0)
    codes = (blocks / scale).astype(np.float32).astype(dtype).astype(np.float64)
    return np.moveaxis((codes * scale).reshape(v.shape), -1, axis)


WIDE = False


def mx_kscale(k):
    if not WIDE:
        return np.ones(k)
    levels = np.array([10, -10, 5, -5, 0])
    if k % 512:
        return np.exp2(np.random.permutation(np.resize(levels, k // 32))).repeat(32)
    a = np.empty((k // 512, 16))
    for p in range(k // 512):
        a[p, :8] = np.random.permutation(np.resize(levels, 8))
        for g in range(8):
            far = levels[np.abs(levels - a[p, g]) >= 10]
            a[p, g + 8] = far[np.random.randint(len(far))]
    return np.exp2(a.ravel()).repeat(32)


def f64(x):
    return np.asarray(x).astype(np.float64)


def striped(idx):
    return np.tile(np.asarray(idx).reshape(-1, 16).T, (8, 1)).astype(np.uint16)


def unstriped(offs):
    return offs[:16].T.reshape(-1).astype(np.int64)


E2M1 = np.array([0.0, 0.5, 1.0, 1.5, 2.0, 3.0, 4.0, 6.0, -0.0, -0.5, -1.0, -1.5, -2.0, -3.0, -4.0, -6.0])


def pack_weight(w, fmt):
    k, n = w.shape
    w = f64(np.asarray(w, np.float32).astype(ml_dtypes.bfloat16)).reshape(k // 32, 32, n)
    amax = np.abs(w).max(1)
    if fmt == "e4m3":
        byte = np.frexp(amax)[1] - 1 + 127 - 7
    else:
        mant, ex = np.frexp(amax / 6.0)
        byte = np.where(mant > 0.5, ex, ex - 1) + 127
    byte = np.clip(np.where(amax > 0, byte, 1), 1, 254)
    scaled = (w * np.exp2(127.0 - byte)[:, None, :]).reshape(k, n).astype(np.float32)
    by_word = np.ascontiguousarray(scaled.reshape(k // 512, 128, 4, n).transpose(0, 1, 3, 2))
    if fmt == "e4m3":
        words = by_word.astype(ml_dtypes.float8_e4m3fn).view(np.uint8)
    else:
        c = by_word.astype(ml_dtypes.float4_e2m1fn).view(np.uint8) & 0xF
        words = (c[..., 0::2] | (c[..., 1::2] << 4)).reshape(k // 512, 128, 2 * n)
    return np.ascontiguousarray(words), np.ascontiguousarray(byte.astype(np.uint8).reshape(k // 512, 16, n))


def unpack_weight(words, scales, fmt):
    g, _, n = scales.shape
    words = np.ascontiguousarray(words).reshape(g, 128, n, -1)
    if fmt == "e4m3":
        vals = words.view(ml_dtypes.float8_e4m3fn).astype(np.float64)
    else:
        nib = np.empty((g, 128, n, 4), np.uint8)
        nib[..., 0::2] = words & 0xF
        nib[..., 1::2] = words >> 4
        vals = E2M1[nib]
    vals = vals * np.repeat(np.exp2(scales.astype(np.float64) - 127.0), 8, axis=1)[..., None]
    return vals.transpose(0, 1, 3, 2).reshape(g * 512, n)


def sigmoid(v):
    return 1.0 / (1.0 + np.exp(-v))


def bf(x):
    return np.asarray(x, np.float32).astype(ml_dtypes.bfloat16)


def planes(Y):
    r, m = Y.shape
    b = f64(bf(Y)).reshape(r // 32, 32, m)
    amax = np.abs(b).max(1)
    byte = np.clip(np.where(amax > 0, np.frexp(amax)[1] - 1 + 127 - 7, 1), 1, 254)
    codes = (b * np.exp2(127.0 - byte)[:, None, :]).reshape(r, m).astype(np.float32).astype(ml_dtypes.float8_e4m3fn).view(np.uint8)
    words = codes.reshape(r // 512, 128, 4, m).transpose(0, 1, 3, 2)
    return np.ascontiguousarray(words), np.ascontiguousarray(byte.astype(np.uint8).reshape(r // 512, 16, m))


K, T, J, N = 1024, 2048, 512, 512


def setup_inputs():
    n = np.random.standard_normal
    idx = np.random.permutation(T)[:J]
    fk = mx_kscale(K)
    wap = pack_weight(n((K, N)) * 1 / np.sqrt(K) * fk[:, None], "e2m1")
    wgp = pack_weight(n((K, N)) * 1 / np.sqrt(K) * fk[:, None], "e4m3")
    whp = pack_weight(n((K, N)) * 1 / np.sqrt(K) * fk[:, None], "e2m1")
    return {
        "xq": (n((K, T)) / fk[:, None]).astype(np.float32),
        "wa_words": wap[0],
        "wa_scales": wap[1],
        "wg_words": wgp[0],
        "wg_scales": wgp[1],
        "wh_words": whp[0],
        "wh_scales": whp[1],
        "offs": striped(idx),
    }


def reference(xq, wa_words, wa_scales, wg_words, wg_scales, wh_words, wh_scales, offs):
    idx = unstriped(offs)
    wau = unpack_weight(wa_words, wa_scales, "e2m1")
    wgu = unpack_weight(wg_words, wg_scales, "e4m3")
    whu = unpack_weight(wh_words, wh_scales, "e2m1")
    xqidxq = mxq(f64(xq)[:, idx], 0, "e4m3")
    p = wau.T @ xqidxq
    g = wgu.T @ xqidxq
    r = whu.T @ xqidxq
    y = np.tanh(p) * sigmoid(g - r)
    words, scales = planes(y)
    return y, words, scales

@@ -1,0 +1,203 @@
+from contextlib import ExitStack
+
+import concourse.mybir as mybir
+
+K, T, J, N = 1024, 2048, 512, 512
+FLOPS = 3 * 2 * K * N * J
+
+F32 = mybir.dt.float32
+BF16 = mybir.dt.bfloat16
+I32 = mybir.dt.int32
+U32 = mybir.dt.uint32
+U16 = mybir.dt.uint16
+U8 = mybir.dt.uint8
+E4M3X4 = mybir.dt.float8_e4m3fn_x4
+E2M1X4 = mybir.dt.float4_e2m1fn_x4
+ACT = mybir.ActivationFunctionType
+MULT = mybir.AluOpType.mult
+
+P = 128
+PACK = 4
+PASSES = K // (P * PACK)
+QUADRANTS = 4
+CHUNK = 128
+CHUNKS = J // CHUNK
+HALF = 256
+HALVES = J // HALF
+WG_ROW = 4
+
+
+def tile_list_competing_gates_pl_kernel(
+    tc, xq, wa_words, wa_scales, wg_words, wg_scales, wh_words, wh_scales, offs, out_0, out_1, out_2
+):
+    nc = tc.nc
+    with ExitStack() as ctx:
+        keep = ctx.enter_context(tc.tile_pool(name="keep", bufs=1))
+        psum = ctx.enter_context(tc.psum_pool(name="psum", bufs=1))
+
+        def sbuf(name, shape, dtype):
+            return keep.tile(shape, dtype, name=name, align_bytes=64)
+
+        offsets = keep.tile([P, J // 16], U16, name="offsets")
+
+        warm_in = sbuf("warm_in", [P, 1], F32)
+        warm_out = sbuf("warm_out", [P, 1], F32)
+        nc.vector.memset(warm_in[:], 0.0)
+        nc.scalar.activation(warm_out[:], warm_in[:], ACT.Sigmoid)
+
+        ag_scale_raw = sbuf("ag_scale_raw", [P, PASSES, N], U8)
+        h_scale_raw = sbuf("h_scale_raw", [P, PASSES, N], U8)
+        nc.gpsimd.memset(ag_scale_raw[:].bitcast(I32), 0)
+        nc.gpsimd.memset(h_scale_raw[:].bitcast(I32), 0)
+
+        wa_raw = sbuf("wa_raw", [P, PASSES, 2 * N], U8)
+        wh_raw = sbuf("wh_raw", [P, PASSES, 2 * N], U8)
+        wg_raw = sbuf("wg_raw", [P, PASSES, 4 * N], U8)
+
+        def load_scale_rows(tile, row, scales):
+            for q in range(QUADRANTS):
+                nc.gpsimd.dma_start(
+                    tile[32 * q + row : 32 * q + row + 4].bitcast(I32),
+                    scales[:, 4 * q : 4 * q + 4, :].rearrange("a r c -> r a c").bitcast(I32),
+                )
+
+        x_rows = xq.rearrange("(a p i) t -> a i p t", a=PASSES, i=PACK)
+        planes = [sbuf("plane%d" % m, [P, T], F32) for m in range(PASSES * PACK)]
+        scale_loads = [(ag_scale_raw, 0, wa_scales), (ag_scale_raw, WG_ROW, wg_scales), (h_scale_raw, 0, wh_scales)]
+        for m, plane in enumerate(planes):
+            nc.sync.dma_start(plane[:], x_rows[m // PACK, m % PACK])
+            if m == 0:
+                nc.sync.dma_start(offsets[:], offs)
+            if m < len(scale_loads):
+                load_scale_rows(*scale_loads[m])
+            if m == 5:
+                nc.sync.dma_start(wa_raw[:].bitcast(I32), wa_words.rearrange("a p c -> p a c").bitcast(I32))
+                nc.sync.dma_start(wg_raw[:].bitcast(I32), wg_words.rearrange("a p n r -> p a (n r)").bitcast(I32))
+                nc.sync.dma_start(wh_raw[:].bitcast(I32), wh_words.rearrange("a p c -> p a c").bitcast(I32))
+
+        def deal(name, raw, dtype, run):
+            dealt = sbuf(name, list(raw[:].shape), U8)
+            nc.vector.tensor_copy(
+                dealt[:].bitcast(dtype).rearrange("p a (t b i) -> p a b t i", t=PACK, i=run),
+                raw[:].bitcast(dtype).rearrange("p a (b i t) -> p a b t i", t=PACK, i=run),
+            )
+            return dealt
+
+
+        def quantise(name, grouped, width):
+            codes = sbuf(name + "_codes", [P, width], U32)
+            scales = sbuf(name + "_scales", [P, width], U8)
+            nc.vector.quantize_mx(
+                out=codes[:].bitcast(E4M3X4), scales=scales[:], in_=grouped[:].rearrange("p j i -> p (j i)")
+            )
+            return codes, scales
+
+        def negate(name, grouped, on_scalar):
+            negated = sbuf(name, [P, HALF, PACK], BF16)
+            if on_scalar:
+                nc.scalar.activation(negated[:], grouped[:], ACT.Copy, scale=-1.0)
+            else:
+                nc.vector.tensor_scalar(negated[:], grouped[:], -1.0, None, MULT)
+            return negated
+
+        def listed(plane, h):
+            return plane[:].indirect(offsets[:, h * HALF // 16 : (h + 1) * HALF // 16])
+
+        def interleave(copy, dst, src):
+            copy(dst.rearrange("p (c i) t -> p c t i", i=4), src.rearrange("p t (c i) -> p c t i", i=4))
+
+        picked = [sbuf("picked%d" % h, [P, PACK, HALF], BF16) for h in range(HALVES)]
+        grouped0 = [sbuf("grouped0_%d" % h, [P, HALF, PACK], BF16) for h in range(HALVES)]
+        for i in range(PACK):
+            for h in range(HALVES):
+                nc.vector.tensor_copy(picked[h][:, i, :], listed(planes[i], h))
+            if i == 0:
+                ag_scale = deal("ag_scale", ag_scale_raw, U8, 16)
+            if i == 2:
+                h_scale = deal("h_scale", h_scale_raw, U8, 16)
+        for h in range(HALVES):
+            interleave(nc.scalar.copy, grouped0[h][:], picked[h][:])
+        negated0 = [negate("negated0_%d" % h, grouped0[h], True) for h in range(HALVES)]
+
+        answer = [psum.tile([P, PACK, CHUNK], F32, name="answer%d" % c) for c in range(CHUNKS)]
+        gate = [psum.tile([P, PACK, CHUNK], F32, name="gate%d" % c) for c in range(CHUNKS)]
+
+        def multiply(bank, words, fmt, w_scales, a, x, x_cols, start, stop):
+            width = words[:].shape[2] // PACK
+            codes, scales = x
+            for t in range(PACK):
+                nc.tensor.matmul_mx(
+                    out=bank[:, t, :],
+                    lhsT=words[:, a, t * width : (t + 1) * width].bitcast(fmt),
+                    lhsT_scale=w_scales[:, a, t * P : (t + 1) * P],
+                    rhs=codes[:, x_cols].bitcast(E4M3X4),
+                    rhs_scale=scales[:, x_cols],
+                    start=start and t == 0,
+                    stop=stop and t == PACK - 1,
+                )
+
+        grouped1 = [sbuf("grouped1_%d" % h, [P, HALF, PACK], BF16) for h in range(HALVES)]
+
+        def gather_last_pass(i, h):
+            nc.vector.tensor_copy(grouped1[h][:, :, i], listed(planes[PACK + i], h))
+
+        def chunks_of(h):
+            per_half = HALF // CHUNK
+            return [(h * per_half + s, slice(s * CHUNK, (s + 1) * CHUNK)) for s in range(per_half)]
+
+        x0 = [quantise("x0_%d" % h, grouped0[h], HALF) for h in range(HALVES)]
+        minus_x0 = [quantise("minus_x0_%d" % h, negated0[h], HALF) for h in range(HALVES)]
+        for i in range(2):
+            for h in range(HALVES):
+                gather_last_pass(i, h)
+        wa = deal("wa", wa_raw, U16, 8)
+        wg = deal("wg", wg_raw, I32, 4)
+        wh = deal("wh", wh_raw, U16, 8)
+        for h in range(HALVES):
+            for c, cols in chunks_of(h):
+                multiply(answer[c], wa, E2M1X4, ag_scale[:], 0, x0[h], cols, True, False)
+        for h in range(HALVES):
+            for c, cols in chunks_of(h):
+                multiply(gate[c], wg, E4M3X4, ag_scale[WG_ROW:P], 0, x0[h], cols, True, False)
+        for h in range(HALVES):
+            for c, cols in chunks_of(h):
+                multiply(gate[c], wh, E2M1X4, h_scale[:], 0, minus_x0[h], cols, False, False)
+        for h in range(HALVES):
+            gather_last_pass(2, h)
+
+        for h in range(HALVES):
+            gather_last_pass(3, h)
+            x1 = quantise("x1_%d" % h, grouped1[h], HALF)
+            negated1 = negate("negated1_%d" % h, grouped1[h], False)
+            minus_x1 = quantise("minus_x1_%d" % h, negated1, HALF)
+            for c, cols in chunks_of(h):
+                multiply(answer[c], wa, E2M1X4, ag_scale[:], 1, x1, cols, False, True)
+                multiply(gate[c], wg, E4M3X4, ag_scale[WG_ROW:P], 1, x1, cols, False, False)
+                multiply(gate[c], wh, E2M1X4, h_scale[:], 1, minus_x1, cols, False, True)
+
+        y_rows = out_0.rearrange("(p t) j -> p t j", t=PACK)
+        y_words = out_1[0].rearrange("p j r -> p (j r)").bitcast(I32)
+        y_scales = sbuf("y_scales", [P, J], U8)
+        for c in range(CHUNKS):
+            cols = slice(c * CHUNK, (c + 1) * CHUNK)
+            tanh_p = sbuf("tanh_p%d" % c, [P, PACK, CHUNK], F32)
+            sigmoid_d = sbuf("sigmoid_d%d" % c, [P, PACK, CHUNK], F32)
+            y = sbuf("y%d" % c, [P, PACK, CHUNK], F32)
+            y_grouped = sbuf("y_grouped%d" % c, [P, CHUNK, PACK], BF16)
+            y_codes = sbuf("y_codes%d" % c, [P, CHUNK], I32)
+            nc.scalar.activation(tanh_p[:], answer[c][:], ACT.Tanh)
+            nc.scalar.activation(sigmoid_d[:], gate[c][:], ACT.Sigmoid)
+            nc.vector.tensor_tensor(y[:], tanh_p[:], sigmoid_d[:], MULT)
+            nc.sync.dma_start(y_rows[:, :, cols], y[:])
+            interleave(nc.vector.tensor_copy, y_grouped[:], y[:])
+            nc.vector.quantize_mx(
+                out=y_codes[:].bitcast(E4M3X4),
+                scales=y_scales[:, cols],
+                in_=y_grouped[:].rearrange("p j t -> p (j t)"),
+            )
+            nc.sync.dma_start(y_words[:, cols], y_codes[:])
+        for q in range(QUADRANTS):
+            queue = nc.sync if q % 2 else nc.scalar
+            queue.dma_start(
+                out_2[0, 4 * q : 4 * q + 4, :].bitcast(I32), y_scales[32 * q : 32 * q + 4, :].bitcast(I32)
+            )

@@ -47,16 +47,16 @@ def tile_list_competing_gates_pl_kernel(
 
         ag_scale_raw = sbuf("ag_scale_raw", [P, PASSES, N], U8)
         h_scale_raw = sbuf("h_scale_raw", [P, PASSES, N], U8)
-        nc.gpsimd.memset(ag_scale_raw[:].bitcast(I32), 0)
-        nc.gpsimd.memset(h_scale_raw[:].bitcast(I32), 0)
+        nc.vector.memset(ag_scale_raw[:].bitcast(I32), 0)
+        nc.vector.memset(h_scale_raw[:].bitcast(I32), 0)
 
         wa_raw = sbuf("wa_raw", [P, PASSES, 2 * N], U8)
-        wh_raw = sbuf("wh_raw", [P, PASSES, 2 * N], U8)
-        wg_raw = sbuf("wg_raw", [P, PASSES, 4 * N], U8)
+        wh_raw = [sbuf("wh_raw%d" % a, [P, 1, 2 * N], U8) for a in range(PASSES)]
+        wg_raw = [sbuf("wg_raw%d" % a, [P, 1, 4 * N], U8) for a in range(PASSES)]
 
         def load_scale_rows(tile, row, scales):
             for q in range(QUADRANTS):
-                nc.gpsimd.dma_start(
+                nc.sync.dma_start(
                     tile[32 * q + row : 32 * q + row + 4].bitcast(I32),
                     scales[:, 4 * q : 4 * q + 4, :].rearrange("a r c -> r a c").bitcast(I32),
                 )
@@ -70,10 +70,13 @@ def tile_list_competing_gates_pl_kernel(
                 nc.sync.dma_start(offsets[:], offs)
             if m < len(scale_loads):
                 load_scale_rows(*scale_loads[m])
-            if m == 5:
+            if m == 4:
                 nc.sync.dma_start(wa_raw[:].bitcast(I32), wa_words.rearrange("a p c -> p a c").bitcast(I32))
-                nc.sync.dma_start(wg_raw[:].bitcast(I32), wg_words.rearrange("a p n r -> p a (n r)").bitcast(I32))
-                nc.sync.dma_start(wh_raw[:].bitcast(I32), wh_words.rearrange("a p c -> p a c").bitcast(I32))
+            if m in (4, 7):
+                a = m // 7
+                nc.sync.dma_start(wg_raw[a][:, 0, :].bitcast(I32), wg_words[a].rearrange("p n r -> p (n r)").bitcast(I32))
+            if m >= 6:
+                nc.sync.dma_start(wh_raw[m - 6][:, 0, :].bitcast(I32), wh_words[m - 6].bitcast(I32))
 
         def deal(name, raw, dtype, run):
             dealt = sbuf(name, list(raw[:].shape), U8)
@@ -128,7 +131,7 @@ def tile_list_competing_gates_pl_kernel(
             for t in range(PACK):
                 nc.tensor.matmul_mx(
                     out=bank[:, t, :],
-                    lhsT=words[:, a, t * width : (t + 1) * width].bitcast(fmt),
+                    lhsT=words[:, a % words[:].shape[1], t * width : (t + 1) * width].bitcast(fmt),
                     lhsT_scale=w_scales[:, a, t * P : (t + 1) * P],
                     rhs=codes[:, x_cols].bitcast(E4M3X4),
                     rhs_scale=scales[:, x_cols],
@@ -147,55 +150,67 @@ def tile_list_competing_gates_pl_kernel(
 
         x0 = [quantise("x0_%d" % h, grouped0[h], HALF) for h in range(HALVES)]
         minus_x0 = [quantise("minus_x0_%d" % h, negated0[h], HALF) for h in range(HALVES)]
-        for i in range(2):
+        for h in range(HALVES):
+            gather_last_pass(0, h)
+        wa = deal("wa", wa_raw, U16, 8)
+        wg0 = deal("wg0", wg_raw[0], I32, 4)
+        for i in (1, 2):
             for h in range(HALVES):
                 gather_last_pass(i, h)
-        wa = deal("wa", wa_raw, U16, 8)
-        wg = deal("wg", wg_raw, I32, 4)
-        wh = deal("wh", wh_raw, U16, 8)
+        wh0 = deal("wh0", wh_raw[0], U16, 8)
         for h in range(HALVES):
             for c, cols in chunks_of(h):
                 multiply(answer[c], wa, E2M1X4, ag_scale[:], 0, x0[h], cols, True, False)
         for h in range(HALVES):
             for c, cols in chunks_of(h):
-                multiply(gate[c], wg, E4M3X4, ag_scale[WG_ROW:P], 0, x0[h], cols, True, False)
+                multiply(gate[c], wg0, E4M3X4, ag_scale[WG_ROW:P], 0, x0[h], cols, True, False)
         for h in range(HALVES):
             for c, cols in chunks_of(h):
-                multiply(gate[c], wh, E2M1X4, h_scale[:], 0, minus_x0[h], cols, False, False)
-        for h in range(HALVES):
-            gather_last_pass(2, h)
+                multiply(gate[c], wh0, E2M1X4, h_scale[:], 0, minus_x0[h], cols, False, False)
 
+        whole = slice(0, CHUNK)
         for h in range(HALVES):
             gather_last_pass(3, h)
-            x1 = quantise("x1_%d" % h, grouped1[h], HALF)
-            negated1 = negate("negated1_%d" % h, grouped1[h], False)
-            minus_x1 = quantise("minus_x1_%d" % h, negated1, HALF)
             for c, cols in chunks_of(h):
-                multiply(answer[c], wa, E2M1X4, ag_scale[:], 1, x1, cols, False, True)
-                multiply(gate[c], wg, E4M3X4, ag_scale[WG_ROW:P], 1, x1, cols, False, False)
-                multiply(gate[c], wh, E2M1X4, h_scale[:], 1, minus_x1, cols, False, True)
+                negated1 = sbuf("negated1_%d" % c, [P, CHUNK, PACK], BF16)
+                nc.vector.tensor_scalar(negated1[:], grouped1[h][:, cols, :], -1.0, None, MULT)
+                x1 = quantise("x1_%d" % c, grouped1[h][:, cols, :], CHUNK)
+                if c == 0:
+                    wg1 = deal("wg1", wg_raw[1], I32, 4)
+                minus_x1 = quantise("minus_x1_%d" % c, negated1, CHUNK)
+                if c == 0:
+                    wh1 = deal("wh1", wh_raw[1], U16, 8)
+                multiply(answer[c], wa, E2M1X4, ag_scale[:], 1, x1, whole, False, True)
+                multiply(gate[c], wg1, E4M3X4, ag_scale[WG_ROW:P], 1, x1, whole, False, False)
+                multiply(gate[c], wh1, E2M1X4, h_scale[:], 1, minus_x1, whole, False, True)
 
         y_rows = out_0.rearrange("(p t) j -> p t j", t=PACK)
         y_words = out_1[0].rearrange("p j r -> p (j r)").bitcast(I32)
         y_scales = sbuf("y_scales", [P, J], U8)
+        y_codes = sbuf("y_codes", [P, J], I32)
         for c in range(CHUNKS):
             cols = slice(c * CHUNK, (c + 1) * CHUNK)
+            last = c == CHUNKS - 1
             tanh_p = sbuf("tanh_p%d" % c, [P, PACK, CHUNK], F32)
             sigmoid_d = sbuf("sigmoid_d%d" % c, [P, PACK, CHUNK], F32)
             y = sbuf("y%d" % c, [P, PACK, CHUNK], F32)
             y_grouped = sbuf("y_grouped%d" % c, [P, CHUNK, PACK], BF16)
-            y_codes = sbuf("y_codes%d" % c, [P, CHUNK], I32)
             nc.scalar.activation(tanh_p[:], answer[c][:], ACT.Tanh)
-            nc.scalar.activation(sigmoid_d[:], gate[c][:], ACT.Sigmoid)
-            nc.vector.tensor_tensor(y[:], tanh_p[:], sigmoid_d[:], MULT)
+            width = CHUNK // 2 if last else CHUNK
+            for first in range(0, CHUNK, width):
+                part = slice(first, first + width)
+                nc.scalar.activation(sigmoid_d[:, :, part], gate[c][:, :, part], ACT.Sigmoid)
+                nc.vector.tensor_tensor(y[:, :, part], tanh_p[:, :, part], sigmoid_d[:, :, part], MULT)
+                interleave(nc.vector.tensor_copy, y_grouped[:, part, :], y[:, :, part])
             nc.sync.dma_start(y_rows[:, :, cols], y[:])
-            interleave(nc.vector.tensor_copy, y_grouped[:], y[:])
             nc.vector.quantize_mx(
-                out=y_codes[:].bitcast(E4M3X4),
+                out=y_codes[:, cols].bitcast(E4M3X4),
                 scales=y_scales[:, cols],
                 in_=y_grouped[:].rearrange("p j t -> p (j t)"),
             )
-            nc.sync.dma_start(y_words[:, cols], y_codes[:])
+            if c >= CHUNKS - 2:
+                done = cols if last else slice(0, J - CHUNK)
+                nc.sync.dma_start(y_words[:, done], y_codes[:, done])
         for q in range(QUADRANTS):
             queue = nc.sync if q % 2 else nc.scalar
             queue.dma_start(

from contextlib import ExitStack

import concourse.mybir as mybir

K, T, J, N = 1024, 2048, 512, 512
FLOPS = 3 * 2 * K * N * J

F32 = mybir.dt.float32
BF16 = mybir.dt.bfloat16
I32 = mybir.dt.int32
U32 = mybir.dt.uint32
U16 = mybir.dt.uint16
U8 = mybir.dt.uint8
E4M3X4 = mybir.dt.float8_e4m3fn_x4
E2M1X4 = mybir.dt.float4_e2m1fn_x4
ACT = mybir.ActivationFunctionType
MULT = mybir.AluOpType.mult

P = 128
PACK = 4
PASSES = K // (P * PACK)
QUADRANTS = 4
CHUNK = 128
CHUNKS = J // CHUNK
HALF = 256
HALVES = J // HALF
WG_ROW = 4


def tile_list_competing_gates_pl_kernel(
    tc, xq, wa_words, wa_scales, wg_words, wg_scales, wh_words, wh_scales, offs, out_0, out_1, out_2
):
    nc = tc.nc
    with ExitStack() as ctx:
        keep = ctx.enter_context(tc.tile_pool(name="keep", bufs=1))
        psum = ctx.enter_context(tc.psum_pool(name="psum", bufs=1))

        def sbuf(name, shape, dtype):
            return keep.tile(shape, dtype, name=name, align_bytes=64)

        offsets = keep.tile([P, J // 16], U16, name="offsets")

        warm_in = sbuf("warm_in", [P, 1], F32)
        warm_out = sbuf("warm_out", [P, 1], F32)
        nc.vector.memset(warm_in[:], 0.0)
        nc.scalar.activation(warm_out[:], warm_in[:], ACT.Sigmoid)

        ag_scale_raw = sbuf("ag_scale_raw", [P, PASSES, N], U8)
        h_scale_raw = sbuf("h_scale_raw", [P, PASSES, N], U8)
        nc.vector.memset(ag_scale_raw[:].bitcast(I32), 0)
        nc.vector.memset(h_scale_raw[:].bitcast(I32), 0)

        wa_raw = sbuf("wa_raw", [P, PASSES, 2 * N], U8)
        wh_raw = [sbuf("wh_raw%d" % a, [P, 1, 2 * N], U8) for a in range(PASSES)]
        wg_raw = [sbuf("wg_raw%d" % a, [P, 1, 4 * N], U8) for a in range(PASSES)]

        def load_scale_rows(tile, row, scales):
            for q in range(QUADRANTS):
                nc.sync.dma_start(
                    tile[32 * q + row : 32 * q + row + 4].bitcast(I32),
                    scales[:, 4 * q : 4 * q + 4, :].rearrange("a r c -> r a c").bitcast(I32),
                )

        x_rows = xq.rearrange("(a p i) t -> a i p t", a=PASSES, i=PACK)
        planes = [sbuf("plane%d" % m, [P, T], F32) for m in range(PASSES * PACK)]
        scale_loads = [(ag_scale_raw, 0, wa_scales), (ag_scale_raw, WG_ROW, wg_scales), (h_scale_raw, 0, wh_scales)]
        for m, plane in enumerate(planes):
            nc.sync.dma_start(plane[:], x_rows[m // PACK, m % PACK])
            if m == 0:
                nc.sync.dma_start(offsets[:], offs)
            if m < len(scale_loads):
                load_scale_rows(*scale_loads[m])
            if m == 4:
                nc.sync.dma_start(wa_raw[:].bitcast(I32), wa_words.rearrange("a p c -> p a c").bitcast(I32))
            if m in (4, 7):
                a = m // 7
                nc.sync.dma_start(wg_raw[a][:, 0, :].bitcast(I32), wg_words[a].rearrange("p n r -> p (n r)").bitcast(I32))
            if m >= 6:
                nc.sync.dma_start(wh_raw[m - 6][:, 0, :].bitcast(I32), wh_words[m - 6].bitcast(I32))

        def deal(name, raw, dtype, run):
            dealt = sbuf(name, list(raw[:].shape), U8)
            nc.vector.tensor_copy(
                dealt[:].bitcast(dtype).rearrange("p a (t b i) -> p a b t i", t=PACK, i=run),
                raw[:].bitcast(dtype).rearrange("p a (b i t) -> p a b t i", t=PACK, i=run),
            )
            return dealt


        def quantise(name, grouped, width):
            codes = sbuf(name + "_codes", [P, width], U32)
            scales = sbuf(name + "_scales", [P, width], U8)
            nc.vector.quantize_mx(
                out=codes[:].bitcast(E4M3X4), scales=scales[:], in_=grouped[:].rearrange("p j i -> p (j i)")
            )
            return codes, scales

        def negate(name, grouped, on_scalar):
            negated = sbuf(name, [P, HALF, PACK], BF16)
            if on_scalar:
                nc.scalar.activation(negated[:], grouped[:], ACT.Copy, scale=-1.0)
            else:
                nc.vector.tensor_scalar(negated[:], grouped[:], -1.0, None, MULT)
            return negated

        def listed(plane, h):
            return plane[:].indirect(offsets[:, h * HALF // 16 : (h + 1) * HALF // 16])

        def interleave(copy, dst, src):
            copy(dst.rearrange("p (c i) t -> p c t i", i=4), src.rearrange("p t (c i) -> p c t i", i=4))

        picked = [sbuf("picked%d" % h, [P, PACK, HALF], BF16) for h in range(HALVES)]
        grouped0 = [sbuf("grouped0_%d" % h, [P, HALF, PACK], BF16) for h in range(HALVES)]
        for i in range(PACK):
            for h in range(HALVES):
                nc.vector.tensor_copy(picked[h][:, i, :], listed(planes[i], h))
            if i == 0:
                ag_scale = deal("ag_scale", ag_scale_raw, U8, 16)
            if i == 2:
                h_scale = deal("h_scale", h_scale_raw, U8, 16)
        for h in range(HALVES):
            interleave(nc.scalar.copy, grouped0[h][:], picked[h][:])
        negated0 = [negate("negated0_%d" % h, grouped0[h], True) for h in range(HALVES)]

        answer = [psum.tile([P, PACK, CHUNK], F32, name="answer%d" % c) for c in range(CHUNKS)]
        gate = [psum.tile([P, PACK, CHUNK], F32, name="gate%d" % c) for c in range(CHUNKS)]

        def multiply(bank, words, fmt, w_scales, a, x, x_cols, start, stop):
            width = words[:].shape[2] // PACK
            codes, scales = x
            for t in range(PACK):
                nc.tensor.matmul_mx(
                    out=bank[:, t, :],
                    lhsT=words[:, a % words[:].shape[1], t * width : (t + 1) * width].bitcast(fmt),
                    lhsT_scale=w_scales[:, a, t * P : (t + 1) * P],
                    rhs=codes[:, x_cols].bitcast(E4M3X4),
                    rhs_scale=scales[:, x_cols],
                    start=start and t == 0,
                    stop=stop and t == PACK - 1,
                )

        grouped1 = [sbuf("grouped1_%d" % h, [P, HALF, PACK], BF16) for h in range(HALVES)]

        def gather_last_pass(i, h):
            nc.vector.tensor_copy(grouped1[h][:, :, i], listed(planes[PACK + i], h))

        def chunks_of(h):
            per_half = HALF // CHUNK
            return [(h * per_half + s, slice(s * CHUNK, (s + 1) * CHUNK)) for s in range(per_half)]

        x0 = [quantise("x0_%d" % h, grouped0[h], HALF) for h in range(HALVES)]
        minus_x0 = [quantise("minus_x0_%d" % h, negated0[h], HALF) for h in range(HALVES)]
        for h in range(HALVES):
            gather_last_pass(0, h)
        wa = deal("wa", wa_raw, U16, 8)
        wg0 = deal("wg0", wg_raw[0], I32, 4)
        for i in (1, 2):
            for h in range(HALVES):
                gather_last_pass(i, h)
        wh0 = deal("wh0", wh_raw[0], U16, 8)
        for h in range(HALVES):
            for c, cols in chunks_of(h):
                multiply(answer[c], wa, E2M1X4, ag_scale[:], 0, x0[h], cols, True, False)
        for h in range(HALVES):
            for c, cols in chunks_of(h):
                multiply(gate[c], wg0, E4M3X4, ag_scale[WG_ROW:P], 0, x0[h], cols, True, False)
        for h in range(HALVES):
            for c, cols in chunks_of(h):
                multiply(gate[c], wh0, E2M1X4, h_scale[:], 0, minus_x0[h], cols, False, False)

        whole = slice(0, CHUNK)
        for h in range(HALVES):
            gather_last_pass(3, h)
            for c, cols in chunks_of(h):
                negated1 = sbuf("negated1_%d" % c, [P, CHUNK, PACK], BF16)
                nc.vector.tensor_scalar(negated1[:], grouped1[h][:, cols, :], -1.0, None, MULT)
                x1 = quantise("x1_%d" % c, grouped1[h][:, cols, :], CHUNK)
                if c == 0:
                    wg1 = deal("wg1", wg_raw[1], I32, 4)
                minus_x1 = quantise("minus_x1_%d" % c, negated1, CHUNK)
                if c == 0:
                    wh1 = deal("wh1", wh_raw[1], U16, 8)
                multiply(answer[c], wa, E2M1X4, ag_scale[:], 1, x1, whole, False, True)
                multiply(gate[c], wg1, E4M3X4, ag_scale[WG_ROW:P], 1, x1, whole, False, False)
                multiply(gate[c], wh1, E2M1X4, h_scale[:], 1, minus_x1, whole, False, True)

        y_rows = out_0.rearrange("(p t) j -> p t j", t=PACK)
        y_words = out_1[0].rearrange("p j r -> p (j r)").bitcast(I32)
        y_scales = sbuf("y_scales", [P, J], U8)
        y_codes = sbuf("y_codes", [P, J], I32)
        for c in range(CHUNKS):
            cols = slice(c * CHUNK, (c + 1) * CHUNK)
            last = c == CHUNKS - 1
            tanh_p = sbuf("tanh_p%d" % c, [P, PACK, CHUNK], F32)
            sigmoid_d = sbuf("sigmoid_d%d" % c, [P, PACK, CHUNK], F32)
            y = sbuf("y%d" % c, [P, PACK, CHUNK], F32)
            y_grouped = sbuf("y_grouped%d" % c, [P, CHUNK, PACK], BF16)
            nc.scalar.activation(tanh_p[:], answer[c][:], ACT.Tanh)
            width = CHUNK // 2 if last else CHUNK
            for first in range(0, CHUNK, width):
                part = slice(first, first + width)
                nc.scalar.activation(sigmoid_d[:, :, part], gate[c][:, :, part], ACT.Sigmoid)
                nc.vector.tensor_tensor(y[:, :, part], tanh_p[:, :, part], sigmoid_d[:, :, part], MULT)
                interleave(nc.vector.tensor_copy, y_grouped[:, part, :], y[:, :, part])
            nc.sync.dma_start(y_rows[:, :, cols], y[:])
            nc.vector.quantize_mx(
                out=y_codes[:, cols].bitcast(E4M3X4),
                scales=y_scales[:, cols],
                in_=y_grouped[:].rearrange("p j t -> p (j t)"),
            )
            if c >= CHUNKS - 2:
                done = cols if last else slice(0, J - CHUNK)
                nc.sync.dma_start(y_words[:, done], y_codes[:, done])
        for q in range(QUADRANTS):
            queue = nc.sync if q % 2 else nc.scalar
            queue.dma_start(
                out_2[0, 4 * q : 4 * q + 4, :].bitcast(I32), y_scales[32 * q : 32 * q + 4, :].bitcast(I32)
            )
